import numpy as np
import ml_dtypes


def mxq(x, axis, fmt="e4m3"):
    dtype, down = {"e4m3": (ml_dtypes.float8_e4m3fn, 7), "e5m2": (ml_dtypes.float8_e5m2, 14)}[fmt]
    v = np.moveaxis(np.asarray(x, np.float32).astype(ml_dtypes.bfloat16).astype(np.float64), axis, -1)
    blocks = v.reshape(v.shape[:-1] + (-1, 32))
    amax = np.abs(blocks).max(-1, keepdims=True)
    byte = np.maximum(np.where(amax > 0, np.frexp(amax)[1] - 1 + 127, 0) - down, 1)
    scale = np.exp2(byte - 127.0)
    codes = (blocks / scale).astype(np.float32).astype(dtype).astype(np.float64)
    return np.moveaxis((codes * scale).reshape(v.shape), -1, axis)


WIDE = False


def mx_kscale(k):
    if not WIDE:
        return np.ones(k)
    levels = np.array([10, -10, 5, -5, 0])
    if k % 512:
        return np.exp2(np.random.permutation(np.resize(levels, k // 32))).repeat(32)
    a = np.empty((k // 512, 16))
    for p in range(k // 512):
        a[p, :8] = np.random.permutation(np.resize(levels, 8))
        for g in range(8):
            far = levels[np.abs(levels - a[p, g]) >= 10]
            a[p, g + 8] = far[np.random.randint(len(far))]
    return np.exp2(a.ravel()).repeat(32)


def f64(x):
    return np.asarray(x).astype(np.float64)


def striped(idx):
    return np.tile(idx.reshape(-1, 16).T, (8, 1)).astype(np.uint16)


def unstriped(offs):
    return offs[:16].T.reshape(-1).astype(np.int64)


E2M1 = np.array([0.0, 0.5, 1.0, 1.5, 2.0, 3.0, 4.0, 6.0, -0.0, -0.5, -1.0, -1.5, -2.0, -3.0, -4.0, -6.0])


def pack_weight(w, fmt):
    k, n = w.shape
    w = f64(np.asarray(w, np.float32).astype(ml_dtypes.bfloat16)).reshape(k // 32, 32, n)
    amax = np.abs(w).max(1)
    if fmt == "e4m3":
        byte = np.frexp(amax)[1] - 1 + 127 - 7
    else:
        mant, ex = np.frexp(amax / 6.0)
        byte = np.where(mant > 0.5, ex, ex - 1) + 127
    byte = np.clip(np.where(amax > 0, byte, 1), 1, 254)
    scaled = (w * np.exp2(127.0 - byte)[:, None, :]).reshape(k, n).astype(np.float32)
    by_word = np.ascontiguousarray(scaled.reshape(k // 512, 128, 4, n).transpose(0, 1, 3, 2))
    if fmt == "e4m3":
        words = by_word.astype(ml_dtypes.float8_e4m3fn).view(np.uint8)
    else:
        c = by_word.astype(ml_dtypes.float4_e2m1fn).view(np.uint8) & 0xF
        words = (c[..., 0::2] | (c[..., 1::2] << 4)).reshape(k // 512, 128, 2 * n)
    return np.ascontiguousarray(words), np.ascontiguousarray(byte.astype(np.uint8).reshape(k // 512, 16, n))


def unpack_weight(words, scales, fmt):
    g, _, n = scales.shape
    words = np.ascontiguousarray(words).reshape(g, 128, n, -1)
    if fmt == "e4m3":
        vals = words.view(ml_dtypes.float8_e4m3fn).astype(np.float64)
    else:
        nib = np.empty((g, 128, n, 4), np.uint8)
        nib[..., 0::2] = words & 0xF
        nib[..., 1::2] = words >> 4
        vals = E2M1[nib]
    vals = vals * np.repeat(np.exp2(scales.astype(np.float64) - 127.0), 8, axis=1)[..., None]
    return vals.transpose(0, 1, 3, 2).reshape(g * 512, n)


def gelu(v):
    return 0.5 * v * (1.0 + np.tanh(np.sqrt(2.0 / np.pi) * (v + 0.044715 * v**3)))


K, T, S, H, T3, S2, P = 1024, 4096, 1024, 512, 2048, 1024, 512

def setup_inputs():
    n = np.random.standard_normal
    s = mx_kscale(K)[:, None]
    u = mx_kscale(H)[:, None]
    d = {}
    d["tab_words"], d["tab_scales"] = pack_weight(n((K, T)) * s, "e4m3")
    d["offs"] = striped(np.random.permutation(T)[:S])
    d["tab2_words"], d["tab2_scales"] = pack_weight(1.2 * n((H, T3)) / H ** 0.5 / u, "e4m3")
    d["offs2"] = striped(np.random.permutation(T3)[:S2])
    d["pos1"] = striped(np.random.permutation(S)[:P])
    d["pos2"] = striped(np.random.permutation(S)[:P])
    d["w1_words"], d["w1_scales"] = pack_weight(1.6 * n((K, H)) / K ** 0.5 / s, "e2m1")
    d["w2"] = (1.5 * n((K, H)) / K ** 0.5 / s * u.T).astype(np.float32)
    d["w3"] = (1.2 * n((K, H)) / K ** 0.5 / s).astype(np.float32)
    d["rv"] = np.exp(0.4 * n(S2)).astype(np.float32)
    return d

def reference(tab_words, tab_scales, offs, tab2_words, tab2_scales, offs2, pos1, pos2,
              w1_words, w1_scales, w2, w3, rv):
    v = unpack_weight(tab_words, tab_scales, "e4m3")[:, unstriped(offs)]
    v2 = unpack_weight(tab2_words, tab2_scales, "e4m3")[:, unstriped(offs2)]
    w1 = unpack_weight(w1_words, w1_scales, "e2m1")
    y1 = w1.T @ v
    y2 = mxq(f64(w2), 0, "e4m3").T @ v
    y3 = mxq(f64(w3), 0, "e4m3").T @ v
    h = y2 / (np.exp(np.tanh(y1)) + np.abs(y3))
    e = v2.T @ mxq(h, 0, "e4m3")
    return np.maximum(e[:, unstriped(pos1)], f64(rv)[:, None] * e[:, unstriped(pos2)])

@@ -1,0 +1,230 @@
+from contextlib import ExitStack
+
+import concourse.mybir as mybir
+from concourse.masks import make_identity
+
+K, T, S, H, T3, S2, PAIRS = 1024, 4096, 1024, 512, 2048, 1024, 512
+FLOPS = 2 * (3 * K * H * S + H * S2 * S)
+
+F32 = mybir.dt.float32
+BF16 = mybir.dt.bfloat16
+I32 = mybir.dt.int32
+U32 = mybir.dt.uint32
+U16 = mybir.dt.uint16
+U8 = mybir.dt.uint8
+E4M3 = mybir.dt.float8_e4m3fn_x4
+E2M1 = mybir.dt.float4_e2m1fn_x4
+ACT = mybir.ActivationFunctionType
+ALU = mybir.AluOpType
+
+P = 128
+PACK = 4
+PASSES = K // (P * PACK)
+CHUNKS = S // P
+HALF = 512
+M_TILES = S2 // P
+QUADS = 4
+KIB = 1024
+TENSOR_ADDS = (0, 1, 2, 3)
+SCALAR_SQUARES = (4, 5, 6, 7)
+
+AT_V0 = (0, 2 * KIB)
+AT_PLANE = 1 * KIB
+AT_W3 = (4 * KIB, 14 * KIB)
+AT_TAB = (12 * KIB, 30 * KIB)
+AT_PLANE2 = 12 * KIB
+AT_TAB2 = 22 * KIB
+AT_W2 = (30 * KIB, 38 * KIB)
+AT_RV = 30 * KIB
+
+
+def tile_list_glaze_firing_scores_kernel(tc, tab_words, tab_scales, offs, tab2_words, tab2_scales, offs2,
+                                                   pos1, pos2, w1_words, w1_scales, w2, w3, rv, out):
+    nc = tc.nc
+    with ExitStack() as ctx:
+        lists = ctx.enter_context(tc.tile_pool(name="lists", bufs=1))
+        arena = ctx.enter_context(tc.tile_pool(name="arena", bufs=1))
+        keep = ctx.enter_context(tc.tile_pool(name="keep", bufs=1))
+        work = ctx.enter_context(tc.tile_pool(name="work", bufs=2))
+        psum = ctx.enter_context(tc.psum_pool(name="psum", bufs=1))
+
+        offs_sb = lists.tile([P, S // 16], U16, name="offs_sb")
+        offs2_sb = lists.tile([P, S2 // 16], U16, name="offs2_sb")
+        pos1_sb = lists.tile([P, PAIRS // 16], U16, name="pos1_sb")
+        pos2_sb = lists.tile([P, PAIRS // 16], U16, name="pos2_sb")
+        for tile, src in ((offs_sb, offs), (offs2_sb, offs2), (pos1_sb, pos1), (pos2_sb, pos2)):
+            nc.sync.dma_start(tile[:], src)
+
+        ident = keep.tile([P, P], F32, name="ident")
+        make_identity(nc, ident[:])
+        rv_rows = arena.tile([P, P], F32, name="rv_rows", offset=AT_RV)
+        nc.vector.memset(rv_rows[:], 0.0)
+        nc.sync.dma_start(rv_rows[0:M_TILES, :], rv.rearrange("(i p) -> i p", p=P))
+        rv_bank = psum.tile([P, HALF], F32, name="rv_bank", tag="y2", bufs=2)
+        nc.tensor.transpose(rv_bank[:, 0:P], rv_rows[:], ident[:])
+        rv_cols = keep.tile([P, M_TILES], F32, name="rv_cols")
+        nc.scalar.activation(rv_cols[:], rv_bank[:, 0:M_TILES], ACT.Copy)
+
+        w1_raw = keep.tile([P, PASSES, 2 * H], U8, name="w1_raw")
+        nc.sync.dma_start(w1_raw[:].bitcast(I32), w1_words.rearrange("a p c -> p a c").bitcast(I32))
+
+        tab_sb = [arena.tile([P, T], I32, name="tab_sb%d" % a, offset=AT_TAB[a]) for a in range(PASSES)]
+
+        def load_tab(a):
+            nc.sync.dma_start(tab_sb[a][:], tab_words[a].rearrange("p t i -> p (t i)").bitcast(I32))
+
+        def load_scale_rows(queue, plane, rows):
+            nc.vector.memset(plane[:].bitcast(I32), 0)
+            for q in range(QUADS):
+                queue.dma_start(plane[32 * q:32 * q + 4].bitcast(I32),
+                                rows[:, 4 * q:4 * q + 4, :].rearrange("a r t -> r a t").bitcast(I32))
+
+        load_tab(0)
+        w1_raw_plane = keep.tile([P, PASSES, H], U8, name="w1_raw_plane")
+        load_scale_rows(nc.gpsimd, w1_raw_plane, w1_scales)
+        tab_plane = arena.tile([P, T], U8, name="tab_plane", offset=AT_PLANE)
+        nc.vector.memset(tab_plane[:].bitcast(I32), 0)
+        for q in range(QUADS):
+            nc.sync.dma_start(tab_plane[32 * q:32 * q + 4 * PASSES, :].bitcast(I32),
+                              tab_scales[:, 4 * q:4 * q + 4, :].bitcast(I32))
+        load_tab(1)
+
+        w1_codes = keep.tile([P, PASSES, 2 * H], U8, name="w1_codes", align_bytes=64)
+        nc.vector.tensor_copy(w1_codes[:].rearrange("p a (t m b) -> p a t m b", t=PACK, b=2),
+                              w1_raw[:].rearrange("p a (m t b) -> p a t m b", t=PACK, b=2))
+        w1_plane = keep.tile([P, PASSES, H], U8, name="w1_plane", align_bytes=64)
+        nc.vector.tensor_copy(w1_plane[:].rearrange("p a (t m) -> p a t m", t=PACK),
+                              w1_raw_plane[:].rearrange("p a (m t) -> p a t m", t=PACK))
+
+        v_scales = [keep.tile([P, S], U8, name="v_scales%d" % a, align_bytes=64) for a in range(PASSES)]
+        nc.vector.memset(v_scales[1][:].bitcast(I32), 0)
+        nc.vector.tensor_copy(v_scales[0][:], tab_plane[:].indirect(offs_sb[:]))
+        for q in range(QUADS):
+            nc.scalar.dma_start(v_scales[1][32 * q:32 * q + 4, :].bitcast(I32),
+                                v_scales[0][32 * q + 4:32 * q + 8, :].bitcast(I32))
+        v_words = {}
+        for a in range(PASSES):
+            for half in range(S // HALF):
+                if a == 0:
+                    v_words[a, half] = arena.tile([P, HALF], U32, name="v_words0_%d" % half, offset=AT_V0[half], align_bytes=64)
+                else:
+                    v_words[a, half] = keep.tile([P, HALF], U32, name="v_words1_%d" % half, align_bytes=64)
+                cols = offs_sb[:, half * HALF // 16:(half + 1) * HALF // 16]
+                nc.vector.tensor_copy(v_words[a, half][:], tab_sb[a][:].bitcast(U32).indirect(cols))
+
+        def v_chunk(a, c):
+            half, first = divmod(c * P, HALF)
+            return v_words[a, half][:, first:first + P].bitcast(E4M3), v_scales[a][:, c * P:(c + 1) * P]
+
+        def quantise_weight(w, name, offsets):
+            codes, scales = [], []
+            for a in range(PASSES):
+                raw = arena.tile([P, PACK, H], F32, name="%s_raw%d" % (name, a), offset=offsets[a])
+                nc.sync.dma_start(raw[:], w[a * P * PACK:(a + 1) * P * PACK, :].rearrange("(p j) c -> p j c", j=PACK))
+                grouped = work.tile([P, H * PACK], BF16, name="grouped", align_bytes=64)
+                nc.vector.tensor_copy(grouped[:].rearrange("p (t m j) -> p m j t", t=PACK, j=PACK),
+                                      raw[:].rearrange("p j (m t) -> p m j t", t=PACK))
+                codes.append(keep.tile([P, H], U32, name="%s_codes%d" % (name, a), align_bytes=64))
+                scales.append(keep.tile([P, H], U8, name="%s_scales%d" % (name, a), align_bytes=64))
+                nc.vector.quantize_mx(codes[a][:].bitcast(E4M3), scales[a][:], grouped[:])
+            return lambda a, cols: (codes[a][:, cols].bitcast(E4M3), scales[a][:, cols])
+
+        def w1_cols(a, cols):
+            return w1_codes[:, a, 2 * cols.start:2 * cols.stop].bitcast(E2M1), w1_plane[:, a, cols]
+
+        w3_cols = quantise_weight(w3, "w3", AT_W3)
+        tab2_plane = arena.tile([P, 1, T3], U8, name="tab2_plane", offset=AT_PLANE2)
+        load_scale_rows(nc.sync, tab2_plane, tab2_scales)
+        tab2_sb = arena.tile([P, T3], I32, name="tab2_sb", offset=AT_TAB2)
+        nc.sync.dma_start(tab2_sb[:], tab2_words[0].rearrange("p t i -> p (t i)").bitcast(I32))
+        w2_cols = quantise_weight(w2, "w2", AT_W2)
+
+        v2_scales = keep.tile([P, S2], U8, name="v2_scales", align_bytes=64)
+        nc.vector.tensor_copy(v2_scales[:], tab2_plane[:, 0, :].indirect(offs2_sb[:]))
+        v2_words = keep.tile([P, S2], U32, name="v2_words", align_bytes=64)
+        nc.vector.tensor_copy(v2_words[:], tab2_sb[:].bitcast(U32).indirect(offs2_sb[:]))
+
+        def woven(bank):
+            return bank[:].rearrange("p (t n) -> p n t", t=PACK)
+
+        def words_of(tile):
+            return tile[:].rearrange("p (n t) -> p n t", t=PACK)
+
+        def product(bank, w_cols, c, turned):
+            for a in range(PASSES):
+                v_codes, v_plane = v_chunk(a, c)
+                if turned:
+                    w_codes, w_plane = w_cols(a, slice(0, H))
+                    nc.tensor.matmul_mx(bank[:], lhsT=v_codes, lhsT_scale=v_plane, rhs=w_codes, rhs_scale=w_plane,
+                                        start=(a == 0), stop=(a == PASSES - 1))
+                else:
+                    for t in range(PACK):
+                        cols = slice(t * P, (t + 1) * P)
+                        w_codes, w_plane = w_cols(a, cols)
+                        nc.tensor.matmul_mx(bank[:, cols], lhsT=w_codes, lhsT_scale=w_plane, rhs=v_codes, rhs_scale=v_plane,
+                                            start=(a == 0 and t == 0), stop=(a == PASSES - 1 and t == PACK - 1))
+
+        def apply(func, tile, bank, turned):
+            if turned:
+                nc.scalar.activation(tile[:], bank[:], func)
+            else:
+                nc.scalar.activation(words_of(tile), woven(bank), func)
+
+        offset_term = []
+        for c in range(CHUNKS):
+            turned = c in TENSOR_ADDS
+            y1 = psum.tile([P, HALF], F32, name="y1", tag="y", bufs=4)
+            product(y1, w1_cols, c, turned)
+            tanh_y1 = work.tile([P, H], F32, name="tanh_y1", tag="s%d" % (c % 3), bufs=1)
+            apply(ACT.Tanh, tanh_y1, y1, turned)
+            offset_term.append(keep.tile([P, H], F32, name="offset_term%d" % c))
+            nc.scalar.activation(offset_term[c][:], tanh_y1[:], ACT.Exp)
+
+        h_codes = [keep.tile([P, HALF], U32, name="h_codes%d" % i, align_bytes=64) for i in range(S // HALF)]
+        h_scales = [keep.tile([P, HALF], U8, name="h_scales%d" % i, align_bytes=64) for i in range(S // HALF)]
+        for c in range(CHUNKS):
+            turned = c in TENSOR_ADDS
+            y3 = psum.tile([P, HALF], F32, name="y3", tag="y", bufs=4)
+            product(y3, w3_cols, c, turned)
+            abs_y3 = work.tile([P, H], F32, name="abs_y3", bufs=4)
+            apply(ACT.Abs, abs_y3, y3, turned)
+            root = work.tile([P, H], F32, name="root", tag="s%d" % ((c + 1) % 3), bufs=1)
+            if turned:
+                denom = psum.tile([P, HALF], F32, name="denom", tag="d", bufs=2)
+                for t in range(PACK):
+                    cols = slice(t * P, (t + 1) * P)
+                    nc.tensor.matmul(denom[:, cols], offset_term[c][:, cols], ident[:], start=True, stop=False, is_transpose=True)
+                    nc.tensor.matmul(denom[:, cols], abs_y3[:, cols], ident[:], start=False, stop=True, is_transpose=True)
+                nc.scalar.activation(words_of(root), woven(denom), ACT.Abs_reciprocal_sqrt)
+            else:
+                denom_sb = work.tile([P, H], F32, name="denom_sb")
+                nc.vector.tensor_tensor(denom_sb[:], offset_term[c][:], abs_y3[:], ALU.add)
+                nc.scalar.activation(root[:], denom_sb[:], ACT.Abs_reciprocal_sqrt)
+            y2 = psum.tile([P, HALF], F32, name="y2", tag="y2", bufs=2)
+            product(y2, w2_cols, c, False)
+            part = work.tile([P, H], F32, name="part")
+            h_bf = work.tile([P, H], BF16, name="h_bf", align_bytes=64)
+            if c in SCALAR_SQUARES:
+                nc.scalar.activation(part[:], root[:], ACT.Square)
+                nc.vector.tensor_tensor(words_of(h_bf), woven(y2), words_of(part), ALU.mult)
+            else:
+                nc.vector.tensor_tensor(words_of(part), woven(y2), words_of(root), ALU.mult)
+                nc.vector.tensor_tensor(h_bf[:], part[:], root[:], ALU.mult)
+            half, first = divmod(c * P, HALF)
+            nc.vector.quantize_mx(h_codes[half][:, first:first + P].bitcast(E4M3), h_scales[half][:, first:first + P], h_bf[:])
+
+        for i in range(M_TILES):
+            rows = slice(i * P, (i + 1) * P)
+            scores = work.tile([P, S], F32, name="scores", bufs=3)
+            for half in range(S // HALF):
+                e = psum.tile([P, HALF], F32, name="e", tag=("y", "d")[half], bufs=(4, 2)[half])
+                nc.tensor.matmul_mx(e[:], lhsT=v2_words[:, rows].bitcast(E4M3), lhsT_scale=v2_scales[:, rows],
+                                    rhs=h_codes[half][:].bitcast(E4M3), rhs_scale=h_scales[half][:], start=True, stop=True)
+                nc.scalar.copy(scores[:, half * HALF:(half + 1) * HALF], e[:])
+            oxidised = work.tile([P, PAIRS], F32, name="oxidised")
+            reduced = work.tile([P, PAIRS], F32, name="reduced")
+            nc.vector.tensor_copy(oxidised[:], scores[:].indirect(pos1_sb[:]))
+            nc.vector.tensor_copy(reduced[:], scores[:].indirect(pos2_sb[:]))
+            best = work.tile([P, PAIRS], F32, name="best", bufs=3)
+            nc.vector.scalar_tensor_tensor(best[:], reduced[:], rv_cols[:, i:i + 1], oxidised[:], ALU.mult, ALU.max)
+            nc.sync.dma_start(out[rows, :], best[:])

@@ -26,16 +26,17 @@ M_TILES = S2 // P
 QUADS = 4
 KIB = 1024
 TENSOR_ADDS = (0, 1, 2, 3)
-SCALAR_SQUARES = (4, 5, 6, 7)
+SCALAR_SQUARES = (2, 3, 4, 5, 6, 7)
 
-AT_V0 = (0, 2 * KIB)
-AT_PLANE = 1 * KIB
-AT_W3 = (4 * KIB, 14 * KIB)
-AT_TAB = (12 * KIB, 30 * KIB)
-AT_PLANE2 = 12 * KIB
-AT_TAB2 = 22 * KIB
-AT_W2 = (30 * KIB, 38 * KIB)
-AT_RV = 30 * KIB
+AT_W3 = (0, 10 * KIB)
+AT_V0 = 8 * KIB
+AT_PLANE = 7 * KIB
+AT_TAB2 = 0
+AT_TAB = (18 * KIB, 34 * KIB)
+AT_PLANE2 = 18 * KIB
+AT_W2 = (34 * KIB, 42 * KIB)
+AT_W1 = 34 * KIB
+AT_RV = 20 * KIB
 
 
 def tile_list_glaze_firing_scores_kernel(tc, tab_words, tab_scales, offs, tab2_words, tab2_scales, offs2,
@@ -55,17 +56,12 @@ def tile_list_glaze_firing_scores_kernel(tc, tab_words, tab_scales, offs, tab2_w
         for tile, src in ((offs_sb, offs), (offs2_sb, offs2), (pos1_sb, pos1), (pos2_sb, pos2)):
             nc.sync.dma_start(tile[:], src)
 
-        ident = keep.tile([P, P], F32, name="ident")
-        make_identity(nc, ident[:])
-        rv_rows = arena.tile([P, P], F32, name="rv_rows", offset=AT_RV)
-        nc.vector.memset(rv_rows[:], 0.0)
-        nc.sync.dma_start(rv_rows[0:M_TILES, :], rv.rearrange("(i p) -> i p", p=P))
-        rv_bank = psum.tile([P, HALF], F32, name="rv_bank", tag="y2", bufs=2)
-        nc.tensor.transpose(rv_bank[:, 0:P], rv_rows[:], ident[:])
-        rv_cols = keep.tile([P, M_TILES], F32, name="rv_cols")
-        nc.scalar.activation(rv_cols[:], rv_bank[:, 0:M_TILES], ACT.Copy)
+        w1_raw_plane = keep.tile([P, PASSES, H], U8, name="w1_raw_plane")
+        nc.vector.memset(w1_raw_plane[:].bitcast(I32), 0)
+        tab_plane = arena.tile([P, T], U8, name="tab_plane", offset=AT_PLANE)
+        nc.vector.memset(tab_plane[:].bitcast(I32), 0)
 
-        w1_raw = keep.tile([P, PASSES, 2 * H], U8, name="w1_raw")
+        w1_raw = arena.tile([P, PASSES, 2 * H], U8, name="w1_raw", offset=AT_W1)
         nc.sync.dma_start(w1_raw[:].bitcast(I32), w1_words.rearrange("a p c -> p a c").bitcast(I32))
 
         tab_sb = [arena.tile([P, T], I32, name="tab_sb%d" % a, offset=AT_TAB[a]) for a in range(PASSES)]
@@ -73,25 +69,23 @@ def tile_list_glaze_firing_scores_kernel(tc, tab_words, tab_scales, offs, tab2_w
         def load_tab(a):
             nc.sync.dma_start(tab_sb[a][:], tab_words[a].rearrange("p t i -> p (t i)").bitcast(I32))
 
-        def load_scale_rows(queue, plane, rows):
-            nc.vector.memset(plane[:].bitcast(I32), 0)
+        def load_scale_rows(queues, plane, rows):
             for q in range(QUADS):
-                queue.dma_start(plane[32 * q:32 * q + 4].bitcast(I32),
+                queues[q].dma_start(plane[32 * q:32 * q + 4].bitcast(I32),
                                 rows[:, 4 * q:4 * q + 4, :].rearrange("a r t -> r a t").bitcast(I32))
 
         load_tab(0)
-        w1_raw_plane = keep.tile([P, PASSES, H], U8, name="w1_raw_plane")
-        load_scale_rows(nc.gpsimd, w1_raw_plane, w1_scales)
-        tab_plane = arena.tile([P, T], U8, name="tab_plane", offset=AT_PLANE)
-        nc.vector.memset(tab_plane[:].bitcast(I32), 0)
+        load_scale_rows((nc.gpsimd, nc.gpsimd, nc.sync, nc.sync), w1_raw_plane, w1_scales)
         for q in range(QUADS):
             nc.sync.dma_start(tab_plane[32 * q:32 * q + 4 * PASSES, :].bitcast(I32),
                               tab_scales[:, 4 * q:4 * q + 4, :].bitcast(I32))
-        load_tab(1)
 
         w1_codes = keep.tile([P, PASSES, 2 * H], U8, name="w1_codes", align_bytes=64)
-        nc.vector.tensor_copy(w1_codes[:].rearrange("p a (t m b) -> p a t m b", t=PACK, b=2),
-                              w1_raw[:].rearrange("p a (m t b) -> p a t m b", t=PACK, b=2))
+        nc.vector.tensor_copy(w1_codes[:].bitcast(U16).rearrange("p a (t m) -> p a t m", t=PACK),
+                              w1_raw[:].bitcast(U16).rearrange("p a (m t) -> p a t m", t=PACK))
+        load_tab(1)
+        ident = keep.tile([P, P], F32, name="ident")
+        make_identity(nc, ident[:])
         w1_plane = keep.tile([P, PASSES, H], U8, name="w1_plane", align_bytes=64)
         nc.vector.tensor_copy(w1_plane[:].rearrange("p a (t m) -> p a t m", t=PACK),
                               w1_raw_plane[:].rearrange("p a (m t) -> p a t m", t=PACK))
@@ -100,15 +94,15 @@ def tile_list_glaze_firing_scores_kernel(tc, tab_words, tab_scales, offs, tab2_w
         nc.vector.memset(v_scales[1][:].bitcast(I32), 0)
         nc.vector.tensor_copy(v_scales[0][:], tab_plane[:].indirect(offs_sb[:]))
         for q in range(QUADS):
-            nc.scalar.dma_start(v_scales[1][32 * q:32 * q + 4, :].bitcast(I32),
+            nc.sync.dma_start(v_scales[1][32 * q:32 * q + 4, :].bitcast(I32),
                                 v_scales[0][32 * q + 4:32 * q + 8, :].bitcast(I32))
         v_words = {}
         for a in range(PASSES):
             for half in range(S // HALF):
-                if a == 0:
-                    v_words[a, half] = arena.tile([P, HALF], U32, name="v_words0_%d" % half, offset=AT_V0[half], align_bytes=64)
+                if (a, half) == (0, 1):
+                    v_words[a, half] = arena.tile([P, HALF], U32, name="v_words0_1", offset=AT_V0, align_bytes=64)
                 else:
-                    v_words[a, half] = keep.tile([P, HALF], U32, name="v_words1_%d" % half, align_bytes=64)
+                    v_words[a, half] = keep.tile([P, HALF], U32, name="v_words%d_%d" % (a, half), align_bytes=64)
                 cols = offs_sb[:, half * HALF // 16:(half + 1) * HALF // 16]
                 nc.vector.tensor_copy(v_words[a, half][:], tab_sb[a][:].bitcast(U32).indirect(cols))
 
@@ -134,15 +128,19 @@ def tile_list_glaze_firing_scores_kernel(tc, tab_words, tab_scales, offs, tab2_w
 
         w3_cols = quantise_weight(w3, "w3", AT_W3)
         tab2_plane = arena.tile([P, 1, T3], U8, name="tab2_plane", offset=AT_PLANE2)
-        load_scale_rows(nc.sync, tab2_plane, tab2_scales)
+        nc.vector.memset(tab2_plane[:].bitcast(I32), 0)
+        load_scale_rows((nc.sync,) * QUADS, tab2_plane, tab2_scales)
+        rv_rows = arena.tile([P, P], F32, name="rv_rows", offset=AT_RV)
+        nc.vector.memset(rv_rows[:], 0.0)
+        nc.sync.dma_start(rv_rows[0:M_TILES, :], rv.rearrange("(i p) -> i p", p=P))
+        rv_bank = psum.tile([P, HALF], F32, name="rv_bank", tag="y2", bufs=2)
+        nc.tensor.transpose(rv_bank[:, 0:P], rv_rows[:], ident[:])
+        rv_cols = keep.tile([P, M_TILES], F32, name="rv_cols")
+        nc.scalar.activation(rv_cols[:], rv_bank[:, 0:M_TILES], ACT.Copy)
+
+        w2_cols = quantise_weight(w2, "w2", AT_W2)
         tab2_sb = arena.tile([P, T3], I32, name="tab2_sb", offset=AT_TAB2)
         nc.sync.dma_start(tab2_sb[:], tab2_words[0].rearrange("p t i -> p (t i)").bitcast(I32))
-        w2_cols = quantise_weight(w2, "w2", AT_W2)
-
-        v2_scales = keep.tile([P, S2], U8, name="v2_scales", align_bytes=64)
-        nc.vector.tensor_copy(v2_scales[:], tab2_plane[:, 0, :].indirect(offs2_sb[:]))
-        v2_words = keep.tile([P, S2], U32, name="v2_words", align_bytes=64)
-        nc.vector.tensor_copy(v2_words[:], tab2_sb[:].bitcast(U32).indirect(offs2_sb[:]))
 
         def woven(bank):
             return bank[:].rearrange("p (t n) -> p n t", t=PACK)
@@ -202,8 +200,8 @@ def tile_list_glaze_firing_scores_kernel(tc, tab_words, tab_scales, offs, tab2_w
                 nc.scalar.activation(root[:], denom_sb[:], ACT.Abs_reciprocal_sqrt)
             y2 = psum.tile([P, HALF], F32, name="y2", tag="y2", bufs=2)
             product(y2, w2_cols, c, False)
-            part = work.tile([P, H], F32, name="part")
-            h_bf = work.tile([P, H], BF16, name="h_bf", align_bytes=64)
+            part = work.tile([P, H], F32, name="part", bufs=3)
+            h_bf = work.tile([P, H], BF16, name="h_bf", tag="hb%d" % (c % 2), bufs=1, align_bytes=64)
             if c in SCALAR_SQUARES:
                 nc.scalar.activation(part[:], root[:], ACT.Square)
                 nc.vector.tensor_tensor(words_of(h_bf), woven(y2), words_of(part), ALU.mult)
@@ -213,12 +211,20 @@ def tile_list_glaze_firing_scores_kernel(tc, tab_words, tab_scales, offs, tab2_w
             half, first = divmod(c * P, HALF)
             nc.vector.quantize_mx(h_codes[half][:, first:first + P].bitcast(E4M3), h_scales[half][:, first:first + P], h_bf[:])
 
+        v2_scales = keep.tile([P, S2], U8, name="v2_scales", align_bytes=64)
+        nc.vector.tensor_copy(v2_scales[:], tab2_plane[:, 0, :].indirect(offs2_sb[:]))
+        v2_words = [keep.tile([P, HALF], U32, name="v2_words0", align_bytes=64),
+                    work.tile([P, HALF], U32, name="v2_words1", tag="hb%d" % ((CHUNKS - 1) % 2), bufs=1, align_bytes=64)]
+        for half in range(S2 // HALF):
+            cols = offs2_sb[:, half * HALF // 16:(half + 1) * HALF // 16]
+            nc.vector.tensor_copy(v2_words[half][:], tab2_sb[:].bitcast(U32).indirect(cols))
+
         for i in range(M_TILES):
             rows = slice(i * P, (i + 1) * P)
             scores = work.tile([P, S], F32, name="scores", bufs=3)
             for half in range(S // HALF):
                 e = psum.tile([P, HALF], F32, name="e", tag=("y", "d")[half], bufs=(4, 2)[half])
-                nc.tensor.matmul_mx(e[:], lhsT=v2_words[:, rows].bitcast(E4M3), lhsT_scale=v2_scales[:, rows],
+                nc.tensor.matmul_mx(e[:], lhsT=v2_words[i * P // HALF][:, i * P % HALF:i * P % HALF + P].bitcast(E4M3), lhsT_scale=v2_scales[:, rows],
                                     rhs=h_codes[half][:].bitcast(E4M3), rhs_scale=h_scales[half][:], start=True, stop=True)
                 nc.scalar.copy(scores[:, half * HALF:(half + 1) * HALF], e[:])
             oxidised = work.tile([P, PAIRS], F32, name="oxidised")

from contextlib import ExitStack

import concourse.mybir as mybir
from concourse.masks import make_identity

K, T, S, H, T3, S2, PAIRS = 1024, 4096, 1024, 512, 2048, 1024, 512
FLOPS = 2 * (3 * K * H * S + H * S2 * S)

F32 = mybir.dt.float32
BF16 = mybir.dt.bfloat16
I32 = mybir.dt.int32
U32 = mybir.dt.uint32
U16 = mybir.dt.uint16
U8 = mybir.dt.uint8
E4M3 = mybir.dt.float8_e4m3fn_x4
E2M1 = mybir.dt.float4_e2m1fn_x4
ACT = mybir.ActivationFunctionType
ALU = mybir.AluOpType

P = 128
PACK = 4
PASSES = K // (P * PACK)
CHUNKS = S // P
HALF = 512
M_TILES = S2 // P
QUADS = 4
KIB = 1024
TENSOR_ADDS = (0, 1, 2, 3)
SCALAR_SQUARES = (2, 3, 4, 5, 6, 7)

AT_W3 = (0, 10 * KIB)
AT_V0 = 8 * KIB
AT_PLANE = 7 * KIB
AT_TAB2 = 0
AT_TAB = (18 * KIB, 34 * KIB)
AT_PLANE2 = 18 * KIB
AT_W2 = (34 * KIB, 42 * KIB)
AT_W1 = 34 * KIB
AT_RV = 20 * KIB


def tile_list_glaze_firing_scores_kernel(tc, tab_words, tab_scales, offs, tab2_words, tab2_scales, offs2,
                                                   pos1, pos2, w1_words, w1_scales, w2, w3, rv, out):
    nc = tc.nc
    with ExitStack() as ctx:
        lists = ctx.enter_context(tc.tile_pool(name="lists", bufs=1))
        arena = ctx.enter_context(tc.tile_pool(name="arena", bufs=1))
        keep = ctx.enter_context(tc.tile_pool(name="keep", bufs=1))
        work = ctx.enter_context(tc.tile_pool(name="work", bufs=2))
        psum = ctx.enter_context(tc.psum_pool(name="psum", bufs=1))

        offs_sb = lists.tile([P, S // 16], U16, name="offs_sb")
        offs2_sb = lists.tile([P, S2 // 16], U16, name="offs2_sb")
        pos1_sb = lists.tile([P, PAIRS // 16], U16, name="pos1_sb")
        pos2_sb = lists.tile([P, PAIRS // 16], U16, name="pos2_sb")
        for tile, src in ((offs_sb, offs), (offs2_sb, offs2), (pos1_sb, pos1), (pos2_sb, pos2)):
            nc.sync.dma_start(tile[:], src)

        w1_raw_plane = keep.tile([P, PASSES, H], U8, name="w1_raw_plane")
        nc.vector.memset(w1_raw_plane[:].bitcast(I32), 0)
        tab_plane = arena.tile([P, T], U8, name="tab_plane", offset=AT_PLANE)
        nc.vector.memset(tab_plane[:].bitcast(I32), 0)

        w1_raw = arena.tile([P, PASSES, 2 * H], U8, name="w1_raw", offset=AT_W1)
        nc.sync.dma_start(w1_raw[:].bitcast(I32), w1_words.rearrange("a p c -> p a c").bitcast(I32))

        tab_sb = [arena.tile([P, T], I32, name="tab_sb%d" % a, offset=AT_TAB[a]) for a in range(PASSES)]

        def load_tab(a):
            nc.sync.dma_start(tab_sb[a][:], tab_words[a].rearrange("p t i -> p (t i)").bitcast(I32))

        def load_scale_rows(queues, plane, rows):
            for q in range(QUADS):
                queues[q].dma_start(plane[32 * q:32 * q + 4].bitcast(I32),
                                rows[:, 4 * q:4 * q + 4, :].rearrange("a r t -> r a t").bitcast(I32))

        load_tab(0)
        load_scale_rows((nc.gpsimd, nc.gpsimd, nc.sync, nc.sync), w1_raw_plane, w1_scales)
        for q in range(QUADS):
            nc.sync.dma_start(tab_plane[32 * q:32 * q + 4 * PASSES, :].bitcast(I32),
                              tab_scales[:, 4 * q:4 * q + 4, :].bitcast(I32))

        w1_codes = keep.tile([P, PASSES, 2 * H], U8, name="w1_codes", align_bytes=64)
        nc.vector.tensor_copy(w1_codes[:].bitcast(U16).rearrange("p a (t m) -> p a t m", t=PACK),
                              w1_raw[:].bitcast(U16).rearrange("p a (m t) -> p a t m", t=PACK))
        load_tab(1)
        ident = keep.tile([P, P], F32, name="ident")
        make_identity(nc, ident[:])
        w1_plane = keep.tile([P, PASSES, H], U8, name="w1_plane", align_bytes=64)
        nc.vector.tensor_copy(w1_plane[:].rearrange("p a (t m) -> p a t m", t=PACK),
                              w1_raw_plane[:].rearrange("p a (m t) -> p a t m", t=PACK))

        v_scales = [keep.tile([P, S], U8, name="v_scales%d" % a, align_bytes=64) for a in range(PASSES)]
        nc.vector.memset(v_scales[1][:].bitcast(I32), 0)
        nc.vector.tensor_copy(v_scales[0][:], tab_plane[:].indirect(offs_sb[:]))
        for q in range(QUADS):
            nc.sync.dma_start(v_scales[1][32 * q:32 * q + 4, :].bitcast(I32),
                                v_scales[0][32 * q + 4:32 * q + 8, :].bitcast(I32))
        v_words = {}
        for a in range(PASSES):
            for half in range(S // HALF):
                if (a, half) == (0, 1):
                    v_words[a, half] = arena.tile([P, HALF], U32, name="v_words0_1", offset=AT_V0, align_bytes=64)
                else:
                    v_words[a, half] = keep.tile([P, HALF], U32, name="v_words%d_%d" % (a, half), align_bytes=64)
                cols = offs_sb[:, half * HALF // 16:(half + 1) * HALF // 16]
                nc.vector.tensor_copy(v_words[a, half][:], tab_sb[a][:].bitcast(U32).indirect(cols))

        def v_chunk(a, c):
            half, first = divmod(c * P, HALF)
            return v_words[a, half][:, first:first + P].bitcast(E4M3), v_scales[a][:, c * P:(c + 1) * P]

        def quantise_weight(w, name, offsets):
            codes, scales = [], []
            for a in range(PASSES):
                raw = arena.tile([P, PACK, H], F32, name="%s_raw%d" % (name, a), offset=offsets[a])
                nc.sync.dma_start(raw[:], w[a * P * PACK:(a + 1) * P * PACK, :].rearrange("(p j) c -> p j c", j=PACK))
                grouped = work.tile([P, H * PACK], BF16, name="grouped", align_bytes=64)
                nc.vector.tensor_copy(grouped[:].rearrange("p (t m j) -> p m j t", t=PACK, j=PACK),
                                      raw[:].rearrange("p j (m t) -> p m j t", t=PACK))
                codes.append(keep.tile([P, H], U32, name="%s_codes%d" % (name, a), align_bytes=64))
                scales.append(keep.tile([P, H], U8, name="%s_scales%d" % (name, a), align_bytes=64))
                nc.vector.quantize_mx(codes[a][:].bitcast(E4M3), scales[a][:], grouped[:])
            return lambda a, cols: (codes[a][:, cols].bitcast(E4M3), scales[a][:, cols])

        def w1_cols(a, cols):
            return w1_codes[:, a, 2 * cols.start:2 * cols.stop].bitcast(E2M1), w1_plane[:, a, cols]

        w3_cols = quantise_weight(w3, "w3", AT_W3)
        tab2_plane = arena.tile([P, 1, T3], U8, name="tab2_plane", offset=AT_PLANE2)
        nc.vector.memset(tab2_plane[:].bitcast(I32), 0)
        load_scale_rows((nc.sync,) * QUADS, tab2_plane, tab2_scales)
        rv_rows = arena.tile([P, P], F32, name="rv_rows", offset=AT_RV)
        nc.vector.memset(rv_rows[:], 0.0)
        nc.sync.dma_start(rv_rows[0:M_TILES, :], rv.rearrange("(i p) -> i p", p=P))
        rv_bank = psum.tile([P, HALF], F32, name="rv_bank", tag="y2", bufs=2)
        nc.tensor.transpose(rv_bank[:, 0:P], rv_rows[:], ident[:])
        rv_cols = keep.tile([P, M_TILES], F32, name="rv_cols")
        nc.scalar.activation(rv_cols[:], rv_bank[:, 0:M_TILES], ACT.Copy)

        w2_cols = quantise_weight(w2, "w2", AT_W2)
        tab2_sb = arena.tile([P, T3], I32, name="tab2_sb", offset=AT_TAB2)
        nc.sync.dma_start(tab2_sb[:], tab2_words[0].rearrange("p t i -> p (t i)").bitcast(I32))

        def woven(bank):
            return bank[:].rearrange("p (t n) -> p n t", t=PACK)

        def words_of(tile):
            return tile[:].rearrange("p (n t) -> p n t", t=PACK)

        def product(bank, w_cols, c, turned):
            for a in range(PASSES):
                v_codes, v_plane = v_chunk(a, c)
                if turned:
                    w_codes, w_plane = w_cols(a, slice(0, H))
                    nc.tensor.matmul_mx(bank[:], lhsT=v_codes, lhsT_scale=v_plane, rhs=w_codes, rhs_scale=w_plane,
                                        start=(a == 0), stop=(a == PASSES - 1))
                else:
                    for t in range(PACK):
                        cols = slice(t * P, (t + 1) * P)
                        w_codes, w_plane = w_cols(a, cols)
                        nc.tensor.matmul_mx(bank[:, cols], lhsT=w_codes, lhsT_scale=w_plane, rhs=v_codes, rhs_scale=v_plane,
                                            start=(a == 0 and t == 0), stop=(a == PASSES - 1 and t == PACK - 1))

        def apply(func, tile, bank, turned):
            if turned:
                nc.scalar.activation(tile[:], bank[:], func)
            else:
                nc.scalar.activation(words_of(tile), woven(bank), func)

        offset_term = []
        for c in range(CHUNKS):
            turned = c in TENSOR_ADDS
            y1 = psum.tile([P, HALF], F32, name="y1", tag="y", bufs=4)
            product(y1, w1_cols, c, turned)
            tanh_y1 = work.tile([P, H], F32, name="tanh_y1", tag="s%d" % (c % 3), bufs=1)
            apply(ACT.Tanh, tanh_y1, y1, turned)
            offset_term.append(keep.tile([P, H], F32, name="offset_term%d" % c))
            nc.scalar.activation(offset_term[c][:], tanh_y1[:], ACT.Exp)

        h_codes = [keep.tile([P, HALF], U32, name="h_codes%d" % i, align_bytes=64) for i in range(S // HALF)]
        h_scales = [keep.tile([P, HALF], U8, name="h_scales%d" % i, align_bytes=64) for i in range(S // HALF)]
        for c in range(CHUNKS):
            turned = c in TENSOR_ADDS
            y3 = psum.tile([P, HALF], F32, name="y3", tag="y", bufs=4)
            product(y3, w3_cols, c, turned)
            abs_y3 = work.tile([P, H], F32, name="abs_y3", bufs=4)
            apply(ACT.Abs, abs_y3, y3, turned)
            root = work.tile([P, H], F32, name="root", tag="s%d" % ((c + 1) % 3), bufs=1)
            if turned:
                denom = psum.tile([P, HALF], F32, name="denom", tag="d", bufs=2)
                for t in range(PACK):
                    cols = slice(t * P, (t + 1) * P)
                    nc.tensor.matmul(denom[:, cols], offset_term[c][:, cols], ident[:], start=True, stop=False, is_transpose=True)
                    nc.tensor.matmul(denom[:, cols], abs_y3[:, cols], ident[:], start=False, stop=True, is_transpose=True)
                nc.scalar.activation(words_of(root), woven(denom), ACT.Abs_reciprocal_sqrt)
            else:
                denom_sb = work.tile([P, H], F32, name="denom_sb")
                nc.vector.tensor_tensor(denom_sb[:], offset_term[c][:], abs_y3[:], ALU.add)
                nc.scalar.activation(root[:], denom_sb[:], ACT.Abs_reciprocal_sqrt)
            y2 = psum.tile([P, HALF], F32, name="y2", tag="y2", bufs=2)
            product(y2, w2_cols, c, False)
            part = work.tile([P, H], F32, name="part", bufs=3)
            h_bf = work.tile([P, H], BF16, name="h_bf", tag="hb%d" % (c % 2), bufs=1, align_bytes=64)
            if c in SCALAR_SQUARES:
                nc.scalar.activation(part[:], root[:], ACT.Square)
                nc.vector.tensor_tensor(words_of(h_bf), woven(y2), words_of(part), ALU.mult)
            else:
                nc.vector.tensor_tensor(words_of(part), woven(y2), words_of(root), ALU.mult)
                nc.vector.tensor_tensor(h_bf[:], part[:], root[:], ALU.mult)
            half, first = divmod(c * P, HALF)
            nc.vector.quantize_mx(h_codes[half][:, first:first + P].bitcast(E4M3), h_scales[half][:, first:first + P], h_bf[:])

        v2_scales = keep.tile([P, S2], U8, name="v2_scales", align_bytes=64)
        nc.vector.tensor_copy(v2_scales[:], tab2_plane[:, 0, :].indirect(offs2_sb[:]))
        v2_words = [keep.tile([P, HALF], U32, name="v2_words0", align_bytes=64),
                    work.tile([P, HALF], U32, name="v2_words1", tag="hb%d" % ((CHUNKS - 1) % 2), bufs=1, align_bytes=64)]
        for half in range(S2 // HALF):
            cols = offs2_sb[:, half * HALF // 16:(half + 1) * HALF // 16]
            nc.vector.tensor_copy(v2_words[half][:], tab2_sb[:].bitcast(U32).indirect(cols))

        for i in range(M_TILES):
            rows = slice(i * P, (i + 1) * P)
            scores = work.tile([P, S], F32, name="scores", bufs=3)
            for half in range(S // HALF):
                e = psum.tile([P, HALF], F32, name="e", tag=("y", "d")[half], bufs=(4, 2)[half])
                nc.tensor.matmul_mx(e[:], lhsT=v2_words[i * P // HALF][:, i * P % HALF:i * P % HALF + P].bitcast(E4M3), lhsT_scale=v2_scales[:, rows],
                                    rhs=h_codes[half][:].bitcast(E4M3), rhs_scale=h_scales[half][:], start=True, stop=True)
                nc.scalar.copy(scores[:, half * HALF:(half + 1) * HALF], e[:])
            oxidised = work.tile([P, PAIRS], F32, name="oxidised")
            reduced = work.tile([P, PAIRS], F32, name="reduced")
            nc.vector.tensor_copy(oxidised[:], scores[:].indirect(pos1_sb[:]))
            nc.vector.tensor_copy(reduced[:], scores[:].indirect(pos2_sb[:]))
            best = work.tile([P, PAIRS], F32, name="best", bufs=3)
            nc.vector.scalar_tensor_tensor(best[:], reduced[:], rv_cols[:, i:i + 1], oxidised[:], ALU.mult, ALU.max)
            nc.sync.dma_start(out[rows, :], best[:])
